import numpy as np
import ml_dtypes


def mxq(x, axis, fmt="e4m3"):
    dtype, down = {"e4m3": (ml_dtypes.float8_e4m3fn, 7), "e5m2": (ml_dtypes.float8_e5m2, 14)}[fmt]
    v = np.moveaxis(np.asarray(x, np.float32).astype(ml_dtypes.bfloat16).astype(np.float64), axis, -1)
    blocks = v.reshape(v.shape[:-1] + (-1, 32))
    amax = np.abs(blocks).max(-1, keepdims=True)
    byte = np.maximum(np.where(amax > 0, np.frexp(amax)[1] - 1 + 127, 0) - down, 1)
    scale = np.exp2(byte - 127.0)
    codes = (blocks / scale).astype(np.float32).astype(dtype).astype(np.float64)
    return np.moveaxis((codes * scale).reshape(v.shape), -1, axis)


WIDE = False


def mx_kscale(k):
    if not WIDE:
        return np.ones(k)
    levels = np.array([10, -10, 5, -5, 0])
    if k % 512:
        return np.exp2(np.random.permutation(np.resize(levels, k // 32))).repeat(32)
    a = np.empty((k // 512, 16))
    for p in range(k // 512):
        a[p, :8] = np.random.permutation(np.resize(levels, 8))
        for g in range(8):
            far = levels[np.abs(levels - a[p, g]) >= 10]
            a[p, g + 8] = far[np.random.randint(len(far))]
    return np.exp2(a.ravel()).repeat(32)


def f64(x):
    return np.asarray(x).astype(np.float64)


def striped(idx):
    return np.tile(np.asarray(idx).reshape(-1, 16).T, (8, 1)).astype(np.uint16)


def unstriped(offs):
    return offs[:16].T.reshape(-1).astype(np.int64)


E2M1 = np.array([0.0, 0.5, 1.0, 1.5, 2.0, 3.0, 4.0, 6.0, -0.0, -0.5, -1.0, -1.5, -2.0, -3.0, -4.0, -6.0])


def pack_weight(w, fmt):
    k, n = w.shape
    w = f64(np.asarray(w, np.float32).astype(ml_dtypes.bfloat16)).reshape(k // 32, 32, n)
    amax = np.abs(w).max(1)
    if fmt == "e4m3":
        byte = np.frexp(amax)[1] - 1 + 127 - 7
    else:
        mant, ex = np.frexp(amax / 6.0)
        byte = np.where(mant > 0.5, ex, ex - 1) + 127
    byte = np.clip(np.where(amax > 0, byte, 1), 1, 254)
    scaled = (w * np.exp2(127.0 - byte)[:, None, :]).reshape(k, n).astype(np.float32)
    by_word = np.ascontiguousarray(scaled.reshape(k // 512, 128, 4, n).transpose(0, 1, 3, 2))
    if fmt == "e4m3":
        words = by_word.astype(ml_dtypes.float8_e4m3fn).view(np.uint8)
    else:
        c = by_word.astype(ml_dtypes.float4_e2m1fn).view(np.uint8) & 0xF
        words = (c[..., 0::2] | (c[..., 1::2] << 4)).reshape(k // 512, 128, 2 * n)
    return np.ascontiguousarray(words), np.ascontiguousarray(byte.astype(np.uint8).reshape(k // 512, 16, n))


def unpack_weight(words, scales, fmt):
    g, _, n = scales.shape
    words = np.ascontiguousarray(words).reshape(g, 128, n, -1)
    if fmt == "e4m3":
        vals = words.view(ml_dtypes.float8_e4m3fn).astype(np.float64)
    else:
        nib = np.empty((g, 128, n, 4), np.uint8)
        nib[..., 0::2] = words & 0xF
        nib[..., 1::2] = words >> 4
        vals = E2M1[nib]
    vals = vals * np.repeat(np.exp2(scales.astype(np.float64) - 127.0), 8, axis=1)[..., None]
    return vals.transpose(0, 1, 3, 2).reshape(g * 512, n)


D, T, I, Q, H, U, G, M = 512, 2048, 512, 128, 512, 1024, 64, 512


def setup_inputs():
    n = np.random.standard_normal
    idx = np.random.permutation(T)[:I]
    idx2 = np.random.permutation(U)[:I]
    idx3 = np.random.permutation(M)[:G]
    fh = mx_kscale(H)
    fd = mx_kscale(D)
    keysp = pack_weight(n((D, T)) / fd[:, None], "e4m3")
    return {
        "query": (n((H, Q)) * 1.0 / np.sqrt(H) / fh[:, None]).astype(np.float32),
        "wk": (n((D, H)) * 0.7 / np.sqrt(D) * fd[:, None] * fh).astype(np.float32),
        "wk2": (n((D, H)) * 0.7 / np.sqrt(D) * fd[:, None] * fh).astype(np.float32),
        "keys_words": keysp[0],
        "keys_scales": keysp[1],
        "parts": (n((D, U)) / fd[:, None]).astype(np.float32),
        "worth": np.tile(np.random.uniform(0.2, 2.0, T), (128, 1)).astype(np.float32),
        "old": (1.0 * n((Q, M))).astype(np.float32),
        "offs": striped(idx),
        "offs2": striped(idx2),
        "offs3": striped(idx3),
    }


def reference(query, wk, wk2, keys_words, keys_scales, parts, worth, old, offs, offs2, offs3):
    idx = unstriped(offs)
    idx2 = unstriped(offs2)
    idx3 = unstriped(offs3)
    keysu = unpack_weight(keys_words, keys_scales, "e4m3")
    wkq = mxq(f64(wk), 0, "e4m3")
    keysidxg = keysu[:, idx]
    wk2q = mxq(f64(wk2), 0, "e4m3")
    partsidx2q = mxq(f64(parts)[:, idx2], 0, "e4m3")
    kp = wkq.T @ keysidxg + wk2q.T @ partsidx2q
    queryq = mxq(f64(query), 0, "e4m3")
    kpq = mxq(kp, 0, "e4m3")
    s = queryq.T @ kpq
    w = np.maximum(s, 0.0)
    ws = w * f64(worth)[:1][:, idx] * 2.0
    wp = ws.reshape(Q, G, I // G).sum(axis=2)
    wf = np.zeros((Q, M))
    wf[:, idx3] = wp
    y = f64(old) + wf
    return y

@@ -1,0 +1,217 @@
+from contextlib import ExitStack
+
+import concourse.mybir as mybir
+from concourse.masks import make_identity
+
+D, T, I, Q, H, U, G, M = 512, 2048, 512, 128, 512, 1024, 64, 512
+FLOPS = 2 * 2 * D * H * I + 2 * H * Q * I
+BYTES = 4 * (H * Q + 2 * D * H + D * U + T + 2 * Q * M) + D * T + 16 * T + 2 * 128 * (32 + 32 + 4)
+
+F32 = mybir.dt.float32
+BF16 = mybir.dt.bfloat16
+I32 = mybir.dt.int32
+U32 = mybir.dt.uint32
+U16 = mybir.dt.uint16
+U8 = mybir.dt.uint8
+FP8X4 = mybir.dt.float8_e4m3fn_x4
+ALU = mybir.AluOpType
+COPY = mybir.ActivationFunctionType.Copy
+
+P = 128
+PACK = 4
+CHUNK = 128
+CHUNKS = I // CHUNK
+HALF = I // 2
+RUN = I // G
+LIST = 16
+
+
+def tile_attend_composedkeys_pagesums_lean_kernel(
+    tc, query, wk, wk2, keys_words, keys_scales, parts, worth, old, offs, offs2, offs3, out
+):
+    nc = tc.nc
+    with ExitStack() as ctx:
+        lists = ctx.enter_context(tc.tile_pool(name="lists", bufs=1))
+        sb = ctx.enter_context(tc.tile_pool(name="sb", bufs=1))
+        ps = ctx.enter_context(tc.psum_pool(name="ps", bufs=1))
+
+        def tile(shape, dtype, name):
+            return sb.tile(shape, dtype, name=name, align_bytes=64)
+
+        def quantize(codes, scales, grouped):
+            nc.vector.quantize_mx(out=codes.bitcast(FP8X4), scales=scales, in_=grouped)
+
+        key_list = lists.tile([P, I // LIST], U16, name="key_list")
+        part_list = lists.tile([P, I // LIST], U16, name="part_list")
+        run_list = lists.tile([P, G // LIST], U16, name="run_list")
+
+        key_scale_pool = tile([P, T], U8, "key_scale_pool")
+        worth_pool = tile([P, T], F32, "worth_pool")
+        placed = tile([P, M], F32, "placed")
+        identity = tile([P, P], F32, "identity")
+        nc.vector.memset(key_scale_pool[:].bitcast(I32), 0)
+        nc.vector.memset(worth_pool[:], 0.0)
+        nc.vector.memset(placed[:], 0.0)
+
+        make_identity(nc, identity[:])
+
+        part_rows = parts.rearrange("(p t) u -> p t u", t=PACK)
+        part_pool = [tile([P, U], F32, "part_pool%d" % t) for t in range(PACK)]
+        wk_raw = tile([P, PACK, H], F32, "wk_raw")
+        wk2_raw = tile([P, PACK, H], F32, "wk2_raw")
+        key_pool = tile([P, T], U32, "key_pool")
+        query_raw = tile([P, PACK, Q], F32, "query_raw")
+        old_sb = tile([P, M], F32, "old_sb")
+
+        nc.sync.dma_start(part_list[:], offs2)
+        nc.sync.dma_start(key_list[:], offs)
+        for t in range(PACK):
+            nc.sync.dma_start(part_pool[t][:], part_rows[:, t, :])
+        for quad in range(4):
+            nc.scalar.dma_start(
+                key_scale_pool[32 * quad : 32 * quad + 4, :].bitcast(I32),
+                keys_scales[0, 4 * quad : 4 * quad + 4, :].bitcast(I32),
+            )
+        nc.scalar.dma_start(worth_pool[0:1, :], worth[0:1, :])
+        nc.sync.dma_start(wk2_raw[:], wk2.rearrange("(p j) h -> p j h", j=PACK))
+        nc.sync.dma_start(wk_raw[:], wk.rearrange("(p j) h -> p j h", j=PACK))
+        nc.sync.dma_start(key_pool[:].bitcast(I32), keys_words[0].rearrange("p n t -> p (n t)").bitcast(I32))
+        nc.sync.dma_start(query_raw[:], query.rearrange("(p j) q -> p j q", j=PACK))
+        nc.sync.dma_start(old_sb[:], old)
+        nc.sync.dma_start(run_list[:], offs3)
+
+        list_halves = [slice(h * HALF // LIST, (h + 1) * HALF // LIST) for h in range(2)]
+        part_planes = [tile([P, PACK, HALF], BF16, "part_planes%d" % h) for h in range(2)]
+        key_scales = tile([P, I], U8, "key_scales")
+
+        def gather_part(t, h, on_vector):
+            picked = part_pool[t][:].indirect(part_list[:, list_halves[h]])
+            if on_vector:
+                nc.vector.tensor_copy(part_planes[h][:, t, :], picked)
+            else:
+                nc.scalar.activation(part_planes[h][:, t, :], picked, COPY)
+
+        for h in range(2):
+            gather_part(0, h, False)
+        nc.vector.tensor_copy(key_scales[:], key_scale_pool[:].indirect(key_list[:]))
+        for h in range(2):
+            gather_part(1, h, False)
+        for h in range(2):
+            gather_part(2, h, True)
+        gather_part(3, 0, True)
+        gather_part(3, 1, False)
+
+        part_codes = [tile([P, HALF], U32, "part_codes%d" % h) for h in range(2)]
+        part_scales = [tile([P, HALF], U8, "part_scales%d" % h) for h in range(2)]
+        part_grouped = [tile([P, HALF * PACK], BF16, "part_grouped%d" % h) for h in range(2)]
+        for h in range(2):
+            nc.vector.tensor_copy(
+                part_grouped[h][:].rearrange("p (c i t) -> p c t i", i=4, t=PACK),
+                part_planes[h][:].rearrange("p t (c i) -> p c t i", i=4),
+            )
+        for h in range(2):
+            quantize(part_codes[h][:], part_scales[h][:], part_grouped[h][:])
+
+        worth_row = tile([P, I], F32, "worth_row")
+        worth_cols = tile([P, CHUNKS], F32, "worth_cols")
+        worth2 = tile([P, I], F32, "worth2")
+        nc.scalar.activation(worth_row[:], worth_pool[:].indirect(key_list[:]), COPY)
+        turned = ps.tile([P, CHUNKS, CHUNK], F32, name="turned")
+        spread = ps.tile([P, CHUNKS, CHUNK], F32, name="spread")
+        for c in range(CHUNKS):
+            nc.tensor.transpose(turned[:, c, :], worth_row[:, c * CHUNK : (c + 1) * CHUNK], identity[:])
+        nc.scalar.copy(worth_cols[:], turned[:, :, 0])
+        for c in range(CHUNKS):
+            nc.tensor.transpose(spread[:, c, :], worth_cols[:, c : c + 1].to_broadcast([P, CHUNK]), identity[:])
+        nc.scalar.activation(worth2[:], spread[:].rearrange("p c s -> p (c s)"), COPY, scale=2.0)
+
+        def quantize_matrix(raw, name):
+            codes = [tile([P, 2 * P], U32, "%s_codes%d" % (name, u)) for u in range(2)]
+            scales = [tile([P, 2 * P], U8, "%s_scales%d" % (name, u)) for u in range(2)]
+            grouped = [tile([P, 2 * P * PACK], BF16, "%s_grouped%d" % (name, u)) for u in range(2)]
+            dealt = raw[:].rearrange("p j (m t) -> p m j t", t=PACK)
+            for u in range(2):
+                dst = grouped[u][:].rearrange("p (t m j) -> p m j t", t=2, j=PACK)
+                src = dealt[:, :, :, 2 * u : 2 * u + 2]
+                if u == 0:
+                    nc.vector.tensor_copy(dst, src)
+                else:
+                    nc.scalar.copy(dst, src)
+            for u in range(2):
+                quantize(codes[u][:], scales[u][:], grouped[u][:])
+            return codes, scales
+
+        banks = [ps.tile([P, PACK, CHUNK], F32, name="kp%d" % c, tag="bank%d" % c) for c in range(CHUNKS)]
+
+        def product(c, w_codes, w_scales, codes, scales, first):
+            for t in range(PACK):
+                cols = slice((t % 2) * P, (t % 2 + 1) * P)
+                nc.tensor.matmul_mx(
+                    out=banks[c][:, t, :],
+                    lhsT=w_codes[t // 2][:, cols].bitcast(FP8X4),
+                    lhsT_scale=w_scales[t // 2][:, cols],
+                    rhs=codes.bitcast(FP8X4),
+                    rhs_scale=scales,
+                    start=(first and t == 0),
+                    stop=(not first and t == PACK - 1),
+                )
+
+        wk2_codes, wk2_scales = quantize_matrix(wk2_raw, "wk2")
+        for c in range(CHUNKS):
+            cols = slice((c % 2) * CHUNK, (c % 2 + 1) * CHUNK)
+            product(c, wk2_codes, wk2_scales, part_codes[c // 2][:, cols], part_scales[c // 2][:, cols], True)
+        wk_codes, wk_scales = quantize_matrix(wk_raw, "wk")
+
+        key_codes = [tile([P, CHUNK], U32, "key_codes%d" % c) for c in range(CHUNKS)]
+        for c in range(CHUNKS):
+            per = CHUNK // LIST
+            nc.vector.tensor_copy(key_codes[c][:], key_pool[:].indirect(key_list[:, c * per : (c + 1) * per]))
+            product(c, wk_codes, wk_scales, key_codes[c][:], key_scales[:, c * CHUNK : (c + 1) * CHUNK], False)
+
+        query_grouped = tile([P, Q * PACK], BF16, "query_grouped")
+        query_codes = tile([P, Q], U32, "query_codes")
+        query_scales = tile([P, Q], U8, "query_scales")
+        nc.scalar.copy(
+            query_grouped[:].rearrange("p (c i t) -> p c t i", i=4, t=PACK),
+            query_raw[:].rearrange("p t (c i) -> p c t i", i=4),
+        )
+        quantize(query_codes[:], query_scales[:], query_grouped[:])
+
+        sums = tile([P, G], F32, "sums")
+        for c in range(CHUNKS):
+            kp_grouped = tile([P, CHUNK * PACK], BF16, "kp_grouped%d" % c)
+            kp_codes = tile([P, CHUNK], U32, "kp_codes%d" % c)
+            kp_scales = tile([P, CHUNK], U8, "kp_scales%d" % c)
+            dst = kp_grouped[:].rearrange("p (s t) -> p s t", t=PACK)
+            src = banks[c][:].rearrange("p t s -> p s t")
+            if c == 2:
+                nc.vector.tensor_copy(dst, src)
+            else:
+                nc.scalar.copy(dst, src)
+            quantize(kp_codes[:], kp_scales[:], kp_grouped[:])
+            scores = ps.tile([P, CHUNK], F32, name="scores%d" % c, tag="bank%d" % c)
+            nc.tensor.matmul_mx(
+                out=scores[:],
+                lhsT=query_codes[:].bitcast(FP8X4),
+                lhsT_scale=query_scales[:],
+                rhs=kp_codes[:].bitcast(FP8X4),
+                rhs_scale=kp_scales[:],
+                start=True,
+                stop=True,
+            )
+            weighted = tile([P, CHUNK], F32, "weighted%d" % c)
+            nc.vector.scalar_tensor_tensor(
+                weighted[:], scores[:], 0.0, worth2[:, c * CHUNK : (c + 1) * CHUNK], ALU.max, ALU.mult
+            )
+            runs = CHUNK // RUN
+            nc.vector.tensor_reduce(
+                sums[:, c * runs : (c + 1) * runs],
+                weighted[:].rearrange("p (g r) -> p g r", r=RUN),
+                mybir.AxisListType.X,
+                ALU.add,
+            )
+
+        result = tile([P, M], F32, "result")
+        nc.vector.tensor_copy(placed[:].indirect(run_list[:]), sums[:])
+        nc.vector.tensor_tensor(result[:], placed[:], old_sb[:], ALU.add)
+        nc.sync.dma_start(out, result[:])

@@ -35,8 +35,8 @@ def tile_attend_composedkeys_pagesums_lean_kernel(
         sb = ctx.enter_context(tc.tile_pool(name="sb", bufs=1))
         ps = ctx.enter_context(tc.psum_pool(name="ps", bufs=1))
 
-        def tile(shape, dtype, name):
-            return sb.tile(shape, dtype, name=name, align_bytes=64)
+        def tile(shape, dtype, name, tag=None):
+            return sb.tile(shape, dtype, name=name, tag=tag or name, align_bytes=64)
 
         def quantize(codes, scales, grouped):
             nc.vector.quantize_mx(out=codes.bitcast(FP8X4), scales=scales, in_=grouped)
@@ -49,8 +49,9 @@ def tile_attend_composedkeys_pagesums_lean_kernel(
         worth_pool = tile([P, T], F32, "worth_pool")
         placed = tile([P, M], F32, "placed")
         identity = tile([P, P], F32, "identity")
-        nc.vector.memset(key_scale_pool[:].bitcast(I32), 0)
-        nc.vector.memset(worth_pool[:], 0.0)
+        nc.gpsimd.memset(key_scale_pool[:].bitcast(I32), 0)
+        nc.gpsimd.memset(worth_pool[:, : T // 2], 0.0)
+        nc.vector.memset(worth_pool[:, T // 2 :], 0.0)
         nc.vector.memset(placed[:], 0.0)
 
         make_identity(nc, identity[:])
@@ -64,15 +65,17 @@ def tile_attend_composedkeys_pagesums_lean_kernel(
         old_sb = tile([P, M], F32, "old_sb")
 
         nc.sync.dma_start(part_list[:], offs2)
+        nc.sync.dma_start(part_pool[0][:], part_rows[:, 0, :])
         nc.sync.dma_start(key_list[:], offs)
-        for t in range(PACK):
-            nc.sync.dma_start(part_pool[t][:], part_rows[:, t, :])
+        nc.sync.dma_start(part_pool[1][:], part_rows[:, 1, :])
         for quad in range(4):
-            nc.scalar.dma_start(
+            nc.sync.dma_start(
                 key_scale_pool[32 * quad : 32 * quad + 4, :].bitcast(I32),
                 keys_scales[0, 4 * quad : 4 * quad + 4, :].bitcast(I32),
             )
         nc.scalar.dma_start(worth_pool[0:1, :], worth[0:1, :])
+        for t in range(2, PACK):
+            nc.sync.dma_start(part_pool[t][:], part_rows[:, t, :])
         nc.sync.dma_start(wk2_raw[:], wk2.rearrange("(p j) h -> p j h", j=PACK))
         nc.sync.dma_start(wk_raw[:], wk.rearrange("(p j) h -> p j h", j=PACK))
         nc.sync.dma_start(key_pool[:].bitcast(I32), keys_words[0].rearrange("p n t -> p (n t)").bitcast(I32))
@@ -91,15 +94,10 @@ def tile_attend_composedkeys_pagesums_lean_kernel(
             else:
                 nc.scalar.activation(part_planes[h][:, t, :], picked, COPY)
 
-        for h in range(2):
-            gather_part(0, h, False)
+        for t in range(PACK):
+            gather_part(t, 0, True)
+            gather_part(t, 1, False)
         nc.vector.tensor_copy(key_scales[:], key_scale_pool[:].indirect(key_list[:]))
-        for h in range(2):
-            gather_part(1, h, False)
-        for h in range(2):
-            gather_part(2, h, True)
-        gather_part(3, 0, True)
-        gather_part(3, 1, False)
 
         part_codes = [tile([P, HALF], U32, "part_codes%d" % h) for h in range(2)]
         part_scales = [tile([P, HALF], U8, "part_scales%d" % h) for h in range(2)]
@@ -112,10 +110,10 @@ def tile_attend_composedkeys_pagesums_lean_kernel(
         for h in range(2):
             quantize(part_codes[h][:], part_scales[h][:], part_grouped[h][:])
 
-        worth_row = tile([P, I], F32, "worth_row")
+        worth_row = tile([P, I], F32, "worth_row", tag="part_pool3")
+        nc.scalar.activation(worth_row[:], worth_pool[:].indirect(key_list[:]), COPY)
         worth_cols = tile([P, CHUNKS], F32, "worth_cols")
         worth2 = tile([P, I], F32, "worth2")
-        nc.scalar.activation(worth_row[:], worth_pool[:].indirect(key_list[:]), COPY)
         turned = ps.tile([P, CHUNKS, CHUNK], F32, name="turned")
         spread = ps.tile([P, CHUNKS, CHUNK], F32, name="spread")
         for c in range(CHUNKS):
@@ -177,41 +175,49 @@ def tile_attend_composedkeys_pagesums_lean_kernel(
         )
         quantize(query_codes[:], query_scales[:], query_grouped[:])
 
+        groups = [(0, 2), (2, 4)]
+        scores = [
+            ps.tile([P, (last - first) * CHUNK], F32, name="scores%d" % first, tag="bank%d" % first)
+            for first, last in groups
+        ]
+        for g, (first, last) in enumerate(groups):
+            for c in range(first, last):
+                kp_grouped = tile([P, CHUNK * PACK], BF16, "kp_grouped%d" % c)
+                kp_codes = tile([P, CHUNK], U32, "kp_codes%d" % c)
+                kp_scales = tile([P, CHUNK], U8, "kp_scales%d" % c)
+                dst = kp_grouped[:].rearrange("p (s t) -> p s t", t=PACK)
+                src = banks[c][:].rearrange("p t s -> p s t")
+                if c == 1:
+                    nc.vector.tensor_copy(dst, src)
+                else:
+                    nc.scalar.copy(dst, src)
+                quantize(kp_codes[:], kp_scales[:], kp_grouped[:])
+                nc.tensor.matmul_mx(
+                    out=scores[g][:, (c - first) * CHUNK : (c - first + 1) * CHUNK],
+                    lhsT=query_codes[:].bitcast(FP8X4),
+                    lhsT_scale=query_scales[:],
+                    rhs=kp_codes[:].bitcast(FP8X4),
+                    rhs_scale=kp_scales[:],
+                    start=True,
+                    stop=True,
+                )
+
         sums = tile([P, G], F32, "sums")
-        for c in range(CHUNKS):
-            kp_grouped = tile([P, CHUNK * PACK], BF16, "kp_grouped%d" % c)
-            kp_codes = tile([P, CHUNK], U32, "kp_codes%d" % c)
-            kp_scales = tile([P, CHUNK], U8, "kp_scales%d" % c)
-            dst = kp_grouped[:].rearrange("p (s t) -> p s t", t=PACK)
-            src = banks[c][:].rearrange("p t s -> p s t")
-            if c == 2:
-                nc.vector.tensor_copy(dst, src)
-            else:
-                nc.scalar.copy(dst, src)
-            quantize(kp_codes[:], kp_scales[:], kp_grouped[:])
-            scores = ps.tile([P, CHUNK], F32, name="scores%d" % c, tag="bank%d" % c)
-            nc.tensor.matmul_mx(
-                out=scores[:],
-                lhsT=query_codes[:].bitcast(FP8X4),
-                lhsT_scale=query_scales[:],
-                rhs=kp_codes[:].bitcast(FP8X4),
-                rhs_scale=kp_scales[:],
-                start=True,
-                stop=True,
-            )
-            weighted = tile([P, CHUNK], F32, "weighted%d" % c)
+        weighted = [tile([P, (last - first) * CHUNK], F32, "weighted%d" % first) for first, last in groups]
+        for g, (first, last) in enumerate(groups):
             nc.vector.scalar_tensor_tensor(
-                weighted[:], scores[:], 0.0, worth2[:, c * CHUNK : (c + 1) * CHUNK], ALU.max, ALU.mult
+                weighted[g][:], scores[g][:], 0.0, worth2[:, first * CHUNK : last * CHUNK], ALU.max, ALU.mult
             )
-            runs = CHUNK // RUN
+        for g, (first, last) in enumerate(groups):
             nc.vector.tensor_reduce(
-                sums[:, c * runs : (c + 1) * runs],
-                weighted[:].rearrange("p (g r) -> p g r", r=RUN),
+                sums[:, first * CHUNK // RUN : last * CHUNK // RUN],
+                weighted[g][:].rearrange("p (g r) -> p g r", r=RUN),
                 mybir.AxisListType.X,
                 ALU.add,
             )
 
         result = tile([P, M], F32, "result")
         nc.vector.tensor_copy(placed[:].indirect(run_list[:]), sums[:])
-        nc.vector.tensor_tensor(result[:], placed[:], old_sb[:], ALU.add)
-        nc.sync.dma_start(out, result[:])
+        for queue, cols in ((nc.scalar, slice(0, M // 2)), (nc.sync, slice(M // 2, M))):
+            nc.vector.tensor_tensor(result[:, cols], placed[:, cols], old_sb[:, cols], ALU.add)
+            queue.dma_start(out[:, cols], result[:, cols])

@@ -49,6 +49,10 @@ def tile_attend_composedkeys_pagesums_lean_kernel(
         worth_pool = tile([P, T], F32, "worth_pool")
         placed = tile([P, M], F32, "placed")
         identity = tile([P, P], F32, "identity")
+        warm_in = tile([P, 1], F32, "warm_in")
+        warm_out = tile([P, 1], F32, "warm_out")
+        nc.vector.memset(warm_in[:], 0.0)
+        nc.scalar.activation(warm_out[:], warm_in[:], COPY)
         nc.gpsimd.memset(key_scale_pool[:].bitcast(I32), 0)
         nc.gpsimd.memset(worth_pool[:, : T // 2], 0.0)
         nc.vector.memset(worth_pool[:, T // 2 :], 0.0)

from contextlib import ExitStack

import concourse.mybir as mybir
from concourse.masks import make_identity

D, T, I, Q, H, U, G, M = 512, 2048, 512, 128, 512, 1024, 64, 512
FLOPS = 2 * 2 * D * H * I + 2 * H * Q * I
BYTES = 4 * (H * Q + 2 * D * H + D * U + T + 2 * Q * M) + D * T + 16 * T + 2 * 128 * (32 + 32 + 4)

F32 = mybir.dt.float32
BF16 = mybir.dt.bfloat16
I32 = mybir.dt.int32
U32 = mybir.dt.uint32
U16 = mybir.dt.uint16
U8 = mybir.dt.uint8
FP8X4 = mybir.dt.float8_e4m3fn_x4
ALU = mybir.AluOpType
COPY = mybir.ActivationFunctionType.Copy

P = 128
PACK = 4
CHUNK = 128
CHUNKS = I // CHUNK
HALF = I // 2
RUN = I // G
LIST = 16


def tile_attend_composedkeys_pagesums_lean_kernel(
    tc, query, wk, wk2, keys_words, keys_scales, parts, worth, old, offs, offs2, offs3, out
):
    nc = tc.nc
    with ExitStack() as ctx:
        lists = ctx.enter_context(tc.tile_pool(name="lists", bufs=1))
        sb = ctx.enter_context(tc.tile_pool(name="sb", bufs=1))
        ps = ctx.enter_context(tc.psum_pool(name="ps", bufs=1))

        def tile(shape, dtype, name, tag=None):
            return sb.tile(shape, dtype, name=name, tag=tag or name, align_bytes=64)

        def quantize(codes, scales, grouped):
            nc.vector.quantize_mx(out=codes.bitcast(FP8X4), scales=scales, in_=grouped)

        key_list = lists.tile([P, I // LIST], U16, name="key_list")
        part_list = lists.tile([P, I // LIST], U16, name="part_list")
        run_list = lists.tile([P, G // LIST], U16, name="run_list")

        key_scale_pool = tile([P, T], U8, "key_scale_pool")
        worth_pool = tile([P, T], F32, "worth_pool")
        placed = tile([P, M], F32, "placed")
        identity = tile([P, P], F32, "identity")
        warm_in = tile([P, 1], F32, "warm_in")
        warm_out = tile([P, 1], F32, "warm_out")
        nc.vector.memset(warm_in[:], 0.0)
        nc.scalar.activation(warm_out[:], warm_in[:], COPY)
        nc.gpsimd.memset(key_scale_pool[:].bitcast(I32), 0)
        nc.gpsimd.memset(worth_pool[:, : T // 2], 0.0)
        nc.vector.memset(worth_pool[:, T // 2 :], 0.0)
        nc.vector.memset(placed[:], 0.0)

        make_identity(nc, identity[:])

        part_rows = parts.rearrange("(p t) u -> p t u", t=PACK)
        part_pool = [tile([P, U], F32, "part_pool%d" % t) for t in range(PACK)]
        wk_raw = tile([P, PACK, H], F32, "wk_raw")
        wk2_raw = tile([P, PACK, H], F32, "wk2_raw")
        key_pool = tile([P, T], U32, "key_pool")
        query_raw = tile([P, PACK, Q], F32, "query_raw")
        old_sb = tile([P, M], F32, "old_sb")

        nc.sync.dma_start(part_list[:], offs2)
        nc.sync.dma_start(part_pool[0][:], part_rows[:, 0, :])
        nc.sync.dma_start(key_list[:], offs)
        nc.sync.dma_start(part_pool[1][:], part_rows[:, 1, :])
        for quad in range(4):
            nc.sync.dma_start(
                key_scale_pool[32 * quad : 32 * quad + 4, :].bitcast(I32),
                keys_scales[0, 4 * quad : 4 * quad + 4, :].bitcast(I32),
            )
        nc.scalar.dma_start(worth_pool[0:1, :], worth[0:1, :])
        for t in range(2, PACK):
            nc.sync.dma_start(part_pool[t][:], part_rows[:, t, :])
        nc.sync.dma_start(wk2_raw[:], wk2.rearrange("(p j) h -> p j h", j=PACK))
        nc.sync.dma_start(wk_raw[:], wk.rearrange("(p j) h -> p j h", j=PACK))
        nc.sync.dma_start(key_pool[:].bitcast(I32), keys_words[0].rearrange("p n t -> p (n t)").bitcast(I32))
        nc.sync.dma_start(query_raw[:], query.rearrange("(p j) q -> p j q", j=PACK))
        nc.sync.dma_start(old_sb[:], old)
        nc.sync.dma_start(run_list[:], offs3)

        list_halves = [slice(h * HALF // LIST, (h + 1) * HALF // LIST) for h in range(2)]
        part_planes = [tile([P, PACK, HALF], BF16, "part_planes%d" % h) for h in range(2)]
        key_scales = tile([P, I], U8, "key_scales")

        def gather_part(t, h, on_vector):
            picked = part_pool[t][:].indirect(part_list[:, list_halves[h]])
            if on_vector:
                nc.vector.tensor_copy(part_planes[h][:, t, :], picked)
            else:
                nc.scalar.activation(part_planes[h][:, t, :], picked, COPY)

        for t in range(PACK):
            gather_part(t, 0, True)
            gather_part(t, 1, False)
        nc.vector.tensor_copy(key_scales[:], key_scale_pool[:].indirect(key_list[:]))

        part_codes = [tile([P, HALF], U32, "part_codes%d" % h) for h in range(2)]
        part_scales = [tile([P, HALF], U8, "part_scales%d" % h) for h in range(2)]
        part_grouped = [tile([P, HALF * PACK], BF16, "part_grouped%d" % h) for h in range(2)]
        for h in range(2):
            nc.vector.tensor_copy(
                part_grouped[h][:].rearrange("p (c i t) -> p c t i", i=4, t=PACK),
                part_planes[h][:].rearrange("p t (c i) -> p c t i", i=4),
            )
        for h in range(2):
            quantize(part_codes[h][:], part_scales[h][:], part_grouped[h][:])

        worth_row = tile([P, I], F32, "worth_row", tag="part_pool3")
        nc.scalar.activation(worth_row[:], worth_pool[:].indirect(key_list[:]), COPY)
        worth_cols = tile([P, CHUNKS], F32, "worth_cols")
        worth2 = tile([P, I], F32, "worth2")
        turned = ps.tile([P, CHUNKS, CHUNK], F32, name="turned")
        spread = ps.tile([P, CHUNKS, CHUNK], F32, name="spread")
        for c in range(CHUNKS):
            nc.tensor.transpose(turned[:, c, :], worth_row[:, c * CHUNK : (c + 1) * CHUNK], identity[:])
        nc.scalar.copy(worth_cols[:], turned[:, :, 0])
        for c in range(CHUNKS):
            nc.tensor.transpose(spread[:, c, :], worth_cols[:, c : c + 1].to_broadcast([P, CHUNK]), identity[:])
        nc.scalar.activation(worth2[:], spread[:].rearrange("p c s -> p (c s)"), COPY, scale=2.0)

        def quantize_matrix(raw, name):
            codes = [tile([P, 2 * P], U32, "%s_codes%d" % (name, u)) for u in range(2)]
            scales = [tile([P, 2 * P], U8, "%s_scales%d" % (name, u)) for u in range(2)]
            grouped = [tile([P, 2 * P * PACK], BF16, "%s_grouped%d" % (name, u)) for u in range(2)]
            dealt = raw[:].rearrange("p j (m t) -> p m j t", t=PACK)
            for u in range(2):
                dst = grouped[u][:].rearrange("p (t m j) -> p m j t", t=2, j=PACK)
                src = dealt[:, :, :, 2 * u : 2 * u + 2]
                if u == 0:
                    nc.vector.tensor_copy(dst, src)
                else:
                    nc.scalar.copy(dst, src)
            for u in range(2):
                quantize(codes[u][:], scales[u][:], grouped[u][:])
            return codes, scales

        banks = [ps.tile([P, PACK, CHUNK], F32, name="kp%d" % c, tag="bank%d" % c) for c in range(CHUNKS)]

        def product(c, w_codes, w_scales, codes, scales, first):
            for t in range(PACK):
                cols = slice((t % 2) * P, (t % 2 + 1) * P)
                nc.tensor.matmul_mx(
                    out=banks[c][:, t, :],
                    lhsT=w_codes[t // 2][:, cols].bitcast(FP8X4),
                    lhsT_scale=w_scales[t // 2][:, cols],
                    rhs=codes.bitcast(FP8X4),
                    rhs_scale=scales,
                    start=(first and t == 0),
                    stop=(not first and t == PACK - 1),
                )

        wk2_codes, wk2_scales = quantize_matrix(wk2_raw, "wk2")
        for c in range(CHUNKS):
            cols = slice((c % 2) * CHUNK, (c % 2 + 1) * CHUNK)
            product(c, wk2_codes, wk2_scales, part_codes[c // 2][:, cols], part_scales[c // 2][:, cols], True)
        wk_codes, wk_scales = quantize_matrix(wk_raw, "wk")

        key_codes = [tile([P, CHUNK], U32, "key_codes%d" % c) for c in range(CHUNKS)]
        for c in range(CHUNKS):
            per = CHUNK // LIST
            nc.vector.tensor_copy(key_codes[c][:], key_pool[:].indirect(key_list[:, c * per : (c + 1) * per]))
            product(c, wk_codes, wk_scales, key_codes[c][:], key_scales[:, c * CHUNK : (c + 1) * CHUNK], False)

        query_grouped = tile([P, Q * PACK], BF16, "query_grouped")
        query_codes = tile([P, Q], U32, "query_codes")
        query_scales = tile([P, Q], U8, "query_scales")
        nc.scalar.copy(
            query_grouped[:].rearrange("p (c i t) -> p c t i", i=4, t=PACK),
            query_raw[:].rearrange("p t (c i) -> p c t i", i=4),
        )
        quantize(query_codes[:], query_scales[:], query_grouped[:])

        groups = [(0, 2), (2, 4)]
        scores = [
            ps.tile([P, (last - first) * CHUNK], F32, name="scores%d" % first, tag="bank%d" % first)
            for first, last in groups
        ]
        for g, (first, last) in enumerate(groups):
            for c in range(first, last):
                kp_grouped = tile([P, CHUNK * PACK], BF16, "kp_grouped%d" % c)
                kp_codes = tile([P, CHUNK], U32, "kp_codes%d" % c)
                kp_scales = tile([P, CHUNK], U8, "kp_scales%d" % c)
                dst = kp_grouped[:].rearrange("p (s t) -> p s t", t=PACK)
                src = banks[c][:].rearrange("p t s -> p s t")
                if c == 1:
                    nc.vector.tensor_copy(dst, src)
                else:
                    nc.scalar.copy(dst, src)
                quantize(kp_codes[:], kp_scales[:], kp_grouped[:])
                nc.tensor.matmul_mx(
                    out=scores[g][:, (c - first) * CHUNK : (c - first + 1) * CHUNK],
                    lhsT=query_codes[:].bitcast(FP8X4),
                    lhsT_scale=query_scales[:],
                    rhs=kp_codes[:].bitcast(FP8X4),
                    rhs_scale=kp_scales[:],
                    start=True,
                    stop=True,
                )

        sums = tile([P, G], F32, "sums")
        weighted = [tile([P, (last - first) * CHUNK], F32, "weighted%d" % first) for first, last in groups]
        for g, (first, last) in enumerate(groups):
            nc.vector.scalar_tensor_tensor(
                weighted[g][:], scores[g][:], 0.0, worth2[:, first * CHUNK : last * CHUNK], ALU.max, ALU.mult
            )
        for g, (first, last) in enumerate(groups):
            nc.vector.tensor_reduce(
                sums[:, first * CHUNK // RUN : last * CHUNK // RUN],
                weighted[g][:].rearrange("p (g r) -> p g r", r=RUN),
                mybir.AxisListType.X,
                ALU.add,
            )

        result = tile([P, M], F32, "result")
        nc.vector.tensor_copy(placed[:].indirect(run_list[:]), sums[:])
        for queue, cols in ((nc.scalar, slice(0, M // 2)), (nc.sync, slice(M // 2, M))):
            nc.vector.tensor_tensor(result[:, cols], placed[:, cols], old_sb[:, cols], ALU.add)
            queue.dma_start(out[:, cols], result[:, cols])
